import numpy as np
import ml_dtypes


def mxq(x, axis, fmt="e4m3"):
    dtype, down = {"e4m3": (ml_dtypes.float8_e4m3fn, 7), "e5m2": (ml_dtypes.float8_e5m2, 14)}[fmt]
    v = np.moveaxis(np.asarray(x, np.float32).astype(ml_dtypes.bfloat16).astype(np.float64), axis, -1)
    blocks = v.reshape(v.shape[:-1] + (-1, 32))
    amax = np.abs(blocks).max(-1, keepdims=True)
    byte = np.maximum(np.where(amax > 0, np.frexp(amax)[1] - 1 + 127, 0) - down, 1)
    scale = np.exp2(byte - 127.0)
    codes = (blocks / scale).astype(np.float32).astype(dtype).astype(np.float64)
    return np.moveaxis((codes * scale).reshape(v.shape), -1, axis)


WIDE = False


def mx_kscale(k):
    if not WIDE:
        return np.ones(k)
    levels = np.array([10, -10, 5, -5, 0])
    if k % 512:
        return np.exp2(np.random.permutation(np.resize(levels, k // 32))).repeat(32)
    a = np.empty((k // 512, 16))
    for p in range(k // 512):
        a[p, :8] = np.random.permutation(np.resize(levels, 8))
        for g in range(8):
            far = levels[np.abs(levels - a[p, g]) >= 10]
            a[p, g + 8] = far[np.random.randint(len(far))]
    return np.exp2(a.ravel()).repeat(32)


def f64(x):
    return np.asarray(x).astype(np.float64)


def striped8(idx):
    return np.asarray(idx).reshape(8, -1, 16).transpose(0, 2, 1).reshape(128, -1).astype(np.uint16)


def unstriped8(offs):
    return offs.reshape(8, 16, -1).transpose(0, 2, 1).reshape(8, -1).astype(np.int64)


def pick8(x, idx, run):
    r = np.arange(len(x))
    return x[r[:, None], idx[r % (8 * run) // run]]


E2M1 = np.array([0.0, 0.5, 1.0, 1.5, 2.0, 3.0, 4.0, 6.0, -0.0, -0.5, -1.0, -1.5, -2.0, -3.0, -4.0, -6.0])


def pack_weight(w, fmt):
    k, n = w.shape
    w = f64(np.asarray(w, np.float32).astype(ml_dtypes.bfloat16)).reshape(k // 32, 32, n)
    amax = np.abs(w).max(1)
    if fmt == "e4m3":
        byte = np.frexp(amax)[1] - 1 + 127 - 7
    else:
        mant, ex = np.frexp(amax / 6.0)
        byte = np.where(mant > 0.5, ex, ex - 1) + 127
    byte = np.clip(np.where(amax > 0, byte, 1), 1, 254)
    scaled = (w * np.exp2(127.0 - byte)[:, None, :]).reshape(k, n).astype(np.float32)
    by_word = np.ascontiguousarray(scaled.reshape(k // 512, 128, 4, n).transpose(0, 1, 3, 2))
    if fmt == "e4m3":
        words = by_word.astype(ml_dtypes.float8_e4m3fn).view(np.uint8)
    else:
        c = by_word.astype(ml_dtypes.float4_e2m1fn).view(np.uint8) & 0xF
        words = (c[..., 0::2] | (c[..., 1::2] << 4)).reshape(k // 512, 128, 2 * n)
    return np.ascontiguousarray(words), np.ascontiguousarray(byte.astype(np.uint8).reshape(k // 512, 16, n))


def unpack_weight(words, scales, fmt):
    g, _, n = scales.shape
    words = np.ascontiguousarray(words).reshape(g, 128, n, -1)
    if fmt == "e4m3":
        vals = words.view(ml_dtypes.float8_e4m3fn).astype(np.float64)
    else:
        nib = np.empty((g, 128, n, 4), np.uint8)
        nib[..., 0::2] = words & 0xF
        nib[..., 1::2] = words >> 4
        vals = E2M1[nib]
    vals = vals * np.repeat(np.exp2(scales.astype(np.float64) - 127.0), 8, axis=1)[..., None]
    return vals.transpose(0, 1, 3, 2).reshape(g * 512, n)


D, T, I, Q, E = 512, 1024, 512, 512, 256


def setup_inputs():
    n = np.random.standard_normal
    idx = np.stack([np.random.permutation(T)[:I] for _ in range(8)])
    idx2 = np.stack([np.random.permutation(T)[:I] for _ in range(8)])
    idx3 = np.stack([np.random.permutation(T)[:I] for _ in range(8)])
    idx4 = np.stack([np.random.permutation(T)[:I] for _ in range(8)])
    idx5 = np.stack([np.random.permutation(T)[:I] for _ in range(8)])
    fd = mx_kscale(D)
    fq = mx_kscale(Q)
    keysp = pack_weight(n((D, T)) / fd[:, None], "e2m1")
    mixp = pack_weight(n((Q, E)) * 1.0 / np.sqrt(Q) / fq[:, None], "e4m3")
    return {
        "query": (n((D, Q)) * 1.0 / np.sqrt(D) * fd[:, None]).astype(np.float32),
        "keys_words": keysp[0],
        "keys_scales": keysp[1],
        "lam": (np.random.uniform(0.4, 1.0, (Q, 1))).astype(np.float32),
        "rowf": (np.random.uniform(0.5, 2.0, (Q, 1)) * fq[:, None]).astype(np.float32),
        "mix_words": mixp[0],
        "mix_scales": mixp[1],
        "offs": striped8(idx),
        "offs2": striped8(idx2),
        "offs3": striped8(idx3),
        "offs4": striped8(idx4),
        "offs5": striped8(idx5),
    }


def reference(query, keys_words, keys_scales, lam, rowf, mix_words, mix_scales, offs, offs2, offs3, offs4, offs5):
    idx = unstriped8(offs)
    idx2 = unstriped8(offs2)
    idx3 = unstriped8(offs3)
    idx4 = unstriped8(offs4)
    idx5 = unstriped8(offs5)
    keysu = unpack_weight(keys_words, keys_scales, "e2m1")
    mixu = unpack_weight(mix_words, mix_scales, "e4m3")
    queryq = mxq(f64(query), 0, "e4m3")
    a = queryq.T @ keysu
    w = pick8(a, idx2, 64) * f64(lam) + pick8(a, idx, 64)
    f1 = np.zeros((Q, T))
    f1[np.arange(Q)[:, None], idx3[np.arange(Q) % 512 // 64]] = w
    c1 = f1 - a
    v = np.minimum(pick8(c1, idx4, 64), pick8(c1, idx5, 64))
    g = v + pick8(a, idx, 64)
    gw = g * f64(rowf)
    gwq = mxq(gw, 0, "e4m3")
    y = mixu.T @ gwq
    return y

@@ -1,0 +1,207 @@
+from contextlib import ExitStack
+
+import concourse.mybir as mybir
+
+D, T, I, Q, E = 512, 1024, 512, 512, 256
+FLOPS = 2 * D * Q * T + 2 * Q * E * I
+
+F32 = mybir.dt.float32
+BF16 = mybir.dt.bfloat16
+I32 = mybir.dt.int32
+U32 = mybir.dt.uint32
+U16 = mybir.dt.uint16
+U8 = mybir.dt.uint8
+FP8X4 = mybir.dt.float8_e4m3fn_x4
+FP4X4 = mybir.dt.float4_e2m1fn_x4
+ALU = mybir.AluOpType
+COPY = mybir.ActivationFunctionType.Copy
+
+P = 128
+PACK = 4
+BANK = 512
+HALF = I // 2
+LIST_COLS = I // 16
+
+
+def tile_attend_lookfar_one_mixed_kernel(
+    tc, query, keys_words, keys_scales, lam, rowf, mix_words, mix_scales, offs, offs2, offs3, offs4, offs5, out
+):
+    nc = tc.nc
+    with ExitStack() as ctx:
+        keep = ctx.enter_context(tc.tile_pool(name="keep", bufs=1))
+        psum = ctx.enter_context(tc.psum_pool(name="psum", bufs=8))
+
+        def sb(name, shape, dtype):
+            return keep.tile(shape, dtype, name=name, align_bytes=64)
+
+        key_plane = sb("key_plane", [P, T], U8)
+        mix_plane = sb("mix_plane", [P, E], U8)
+        placed = [sb("placed%d" % b, [P, T], F32) for b in range(2)]
+        nc.vector.memset(key_plane[:].bitcast(I32), 0)
+        nc.vector.memset(mix_plane[:].bitcast(I32), 0)
+        for b in range(2):
+            nc.vector.memset(placed[b][:], 0.0)
+
+        for quad in range(4):
+            nc.scalar.dma_start(
+                out=key_plane[32 * quad : 32 * quad + 4, :].bitcast(I32),
+                in_=keys_scales[0, 4 * quad : 4 * quad + 4, :].bitcast(I32),
+            )
+        q_rows = query.rearrange("(p j) q -> p j q", j=PACK)
+        q_raw = []
+        for c in range(2):
+            raw = sb("q_raw%d" % c, [P, PACK, Q // 2], F32)
+            nc.sync.dma_start(out=raw[:], in_=q_rows[:, :, c * (Q // 2) : (c + 1) * (Q // 2)])
+            q_raw.append(raw)
+        key_words = sb("key_words", [P, 2 * T], U8)
+        nc.sync.dma_start(out=key_words[:].bitcast(I32), in_=keys_words[0].bitcast(I32))
+
+        def load_list(name, src):
+            tile = sb(name, [P, LIST_COLS], U16)
+            nc.sync.dma_start(tile[:], src)
+            return tile
+
+        near = load_list("near", offs)
+        far = load_list("far", offs2)
+        lam_sb = sb("lam_sb", [P, PACK], F32)
+        nc.sync.dma_start(out=lam_sb[:], in_=lam.rearrange("(p r) o -> p (r o)", r=PACK))
+        place = load_list("place", offs3)
+        left = load_list("left", offs4)
+        right = load_list("right", offs5)
+        rowf_sb = sb("rowf_sb", [P, PACK], F32)
+        nc.sync.dma_start(out=rowf_sb[:], in_=rowf.rearrange("(p r) o -> p (r o)", r=PACK))
+        mix_codes = sb("mix_codes", [P, E], U32)
+        nc.sync.dma_start(out=mix_codes[:].bitcast(I32), in_=mix_words[0].rearrange("p n t -> p (n t)").bitcast(I32))
+        for quad in range(4):
+            nc.sync.dma_start(
+                out=mix_plane[32 * quad : 32 * quad + 4, :].bitcast(I32),
+                in_=mix_scales[0, 4 * quad : 4 * quad + 4, :].bitcast(I32),
+            )
+
+        q_bf = [sb("q_bf%d" % u, [P, 2, P, PACK], BF16) for u in range(2)]
+        for c in range(2):
+            src = q_raw[c][:].rearrange("p j (m r) -> p m j r", r=PACK)
+            for u in range(2):
+                dst = q_bf[u][:, :, c * 64 : (c + 1) * 64, :].rearrange("p r m j -> p m j r")
+                if u == 0:
+                    nc.vector.tensor_copy(out=dst, in_=src[:, :, :, 0:2])
+                else:
+                    nc.scalar.activation(out=dst, in_=src[:, :, :, 2:4], func=COPY)
+        q_codes, q_plane = [], []
+        for name, tiles in (("a", (0,)), ("b", (1,)), ("c", (2, 3))):
+            n = len(tiles)
+            codes = sb("q_codes_" + name, [P, n * P], U32)
+            plane = sb("q_plane_" + name, [P, n * P], U8)
+            u, first = divmod(tiles[0], 2)
+            nc.vector.quantize_mx(
+                out=codes[:].bitcast(FP8X4),
+                scales=plane[:],
+                in_=q_bf[u][:, first : first + n].rearrange("p r m j -> p (r m j)"),
+            )
+            for k in range(n):
+                q_codes.append(codes[:, k * P : (k + 1) * P])
+                q_plane.append(plane[:, k * P : (k + 1) * P])
+
+        banks = []
+        for r in range(PACK):
+            for h in range(2):
+                bank = psum.tile([P, BANK], F32, name="bank")
+                nc.tensor.matmul_mx(
+                    out=bank[:],
+                    lhsT=q_codes[r].bitcast(FP8X4),
+                    lhsT_scale=q_plane[r],
+                    rhs=key_words[:, 2 * BANK * h : 2 * BANK * (h + 1)].bitcast(FP4X4),
+                    rhs_scale=key_plane[:, BANK * h : BANK * (h + 1)],
+                    start=True,
+                    stop=True,
+                )
+                banks.append(bank)
+
+        a_near, c1 = [], []
+        for r in range(PACK):
+            a = sb("a%d" % r, [P, T], F32)
+            nc.scalar.copy(out=a[:, 0:BANK], in_=banks[2 * r][:])
+            if r == 0:
+                nc.vector.tensor_copy(out=a[:, BANK:T], in_=banks[2 * r + 1][:])
+            else:
+                nc.scalar.copy(out=a[:, BANK:T], in_=banks[2 * r + 1][:])
+            an = sb("a_near%d" % r, [P, I], F32)
+            af = sb("a_far%d" % r, [P, I], F32)
+            afl = sb("a_far_lam%d" % r, [P, I], F32)
+            nc.scalar.activation(out=an[:], in_=a[:].indirect(near[:]), func=COPY)
+            if r == 0:
+                nc.vector.tensor_copy(out=af[:], in_=a[:].indirect(far[:]))
+                nc.vector.tensor_scalar(out=afl[:], in0=af[:], scalar1=lam_sb[:, r : r + 1], scalar2=None, op0=ALU.mult)
+            else:
+                nc.scalar.activation(out=af[:], in_=a[:].indirect(far[:]), func=COPY)
+                nc.scalar.activation(out=afl[:], in_=af[:], func=COPY, scale=lam_sb[:, r : r + 1])
+            f1 = placed[r % 2]
+            nc.vector.tensor_tensor(out=f1[:].indirect(place[:]), in0=afl[:], in1=an[:], op=ALU.add)
+            c = sb("c%d" % r, [P, T], F32)
+            nc.vector.tensor_tensor(out=c[:], in0=f1[:], in1=a[:], op=ALU.subtract)
+            a_near.append(an)
+            c1.append(c)
+
+        last = PACK - 1
+        pieces = [(r, 0, I) for r in range(last)] + [(last, 0, HALF), (last, HALF, I)]
+        picked = []
+        for r, lo, hi in pieces:
+            cl = sb("c_left%d_%d" % (r, lo), [P, hi - lo], F32)
+            cr = sb("c_right%d_%d" % (r, lo), [P, hi - lo], F32)
+            nc.scalar.activation(out=cl[:], in_=c1[r][:].indirect(left[:, lo // 16 : hi // 16]), func=COPY)
+            nc.scalar.activation(out=cr[:], in_=c1[r][:].indirect(right[:, lo // 16 : hi // 16]), func=COPY)
+            picked.append((cl, cr))
+        gw = sb("gw", [P, 2, PACK, HALF], BF16)
+        sums = []
+        for (r, lo, hi), (cl, cr) in zip(pieces, picked):
+            v = sb("v%d_%d" % (r, lo), [P, hi - lo], F32)
+            g = sb("g%d_%d" % (r, lo), [P, hi - lo], F32)
+            nc.vector.tensor_tensor(out=v[:], in0=cl[:], in1=cr[:], op=ALU.min)
+            nc.vector.tensor_tensor(out=g[:], in0=v[:], in1=a_near[r][:, lo:hi], op=ALU.add)
+            sums.append(g)
+        for (r, lo, hi), g in zip(pieces, sums):
+            if r < last:
+                nc.scalar.activation(
+                    out=gw[:, :, r, :],
+                    in_=g[:].rearrange("p (h i) -> p h i", h=2),
+                    func=COPY,
+                    scale=rowf_sb[:, r : r + 1],
+                )
+            else:
+                nc.vector.tensor_scalar(
+                    out=gw[:, lo // HALF, r, :], in0=g[:], scalar1=rowf_sb[:, r : r + 1], scalar2=None, op0=ALU.mult
+                )
+
+        woven = []
+        for h in range(2):
+            w = sb("woven%d" % h, [P, HALF, PACK], BF16)
+            nc.vector.tensor_copy(
+                out=w[:].rearrange("p (c i) r -> p c r i", i=4),
+                in_=gw[:, h].rearrange("p r (c i) -> p c r i", i=4),
+            )
+            woven.append(w)
+        for h in range(2):
+            codes = sb("g_codes%d" % h, [P, HALF], U32)
+            plane = sb("g_plane%d" % h, [P, HALF], U8)
+            nc.vector.quantize_mx(
+                out=codes[:].bitcast(FP8X4), scales=plane[:], in_=woven[h][:].rearrange("p i r -> p (i r)")
+            )
+            for b in range(E // P):
+                bank = psum.tile([P, BANK], F32, name="bank")
+                nc.tensor.matmul_mx(
+                    out=bank[:, 0:HALF],
+                    lhsT=mix_codes[:, b * P : (b + 1) * P].bitcast(FP8X4),
+                    lhsT_scale=mix_plane[:, b * P : (b + 1) * P],
+                    rhs=codes[:].bitcast(FP8X4),
+                    rhs_scale=plane[:],
+                    start=True,
+                    stop=True,
+                )
+                y = sb("y%d_%d" % (h, b), [P, HALF], F32)
+                dst = out[b * P : (b + 1) * P, h * HALF : (h + 1) * HALF]
+                if h == 1 and b == 1:
+                    nc.vector.tensor_copy(out=y[:], in_=bank[:, 0:HALF])
+                    nc.sync.dma_start(out=dst, in_=y[:])
+                else:
+                    nc.scalar.copy(out=y[:], in_=bank[:, 0:HALF])
+                    nc.sync.dma_start(out=dst, in_=y[:])

@@ -21,6 +21,9 @@ PACK = 4
 BANK = 512
 HALF = I // 2
 LIST_COLS = I // 16
+SPLIT = 704
+BANK_BYTES = 2048
+QUARTER = T // 4
 
 
 def tile_attend_lookfar_one_mixed_kernel(
@@ -29,7 +32,7 @@ def tile_attend_lookfar_one_mixed_kernel(
     nc = tc.nc
     with ExitStack() as ctx:
         keep = ctx.enter_context(tc.tile_pool(name="keep", bufs=1))
-        psum = ctx.enter_context(tc.psum_pool(name="psum", bufs=8))
+        psum = ctx.enter_context(tc.psum_pool(name="psum", bufs=1))
 
         def sb(name, shape, dtype):
             return keep.tile(shape, dtype, name=name, align_bytes=64)
@@ -37,7 +40,7 @@ def tile_attend_lookfar_one_mixed_kernel(
         key_plane = sb("key_plane", [P, T], U8)
         mix_plane = sb("mix_plane", [P, E], U8)
         placed = [sb("placed%d" % b, [P, T], F32) for b in range(2)]
-        nc.vector.memset(key_plane[:].bitcast(I32), 0)
+        nc.gpsimd.memset(key_plane[:].bitcast(I32), 0)
         nc.vector.memset(mix_plane[:].bitcast(I32), 0)
         for b in range(2):
             nc.vector.memset(placed[b][:], 0.0)
@@ -102,12 +105,11 @@ def tile_attend_lookfar_one_mixed_kernel(
                 q_codes.append(codes[:, k * P : (k + 1) * P])
                 q_plane.append(plane[:, k * P : (k + 1) * P])
 
-        banks = []
-        for r in range(PACK):
+        def scores(r):
+            pair = psum.tile([P, T], F32, name="pair%d" % r, offset=2 * BANK_BYTES * ((r + 1) % 2))
             for h in range(2):
-                bank = psum.tile([P, BANK], F32, name="bank")
                 nc.tensor.matmul_mx(
-                    out=bank[:],
+                    out=pair[:, BANK * h : BANK * (h + 1)],
                     lhsT=q_codes[r].bitcast(FP8X4),
                     lhsT_scale=q_plane[r],
                     rhs=key_words[:, 2 * BANK * h : 2 * BANK * (h + 1)].bitcast(FP4X4),
@@ -115,62 +117,99 @@ def tile_attend_lookfar_one_mixed_kernel(
                     start=True,
                     stop=True,
                 )
-                banks.append(bank)
+            return pair
 
-        a_near, c1 = [], []
+        last = PACK - 1
+        a_near, c1, a_sb = [], [], []
+
+        def shared(name, r, width):
+            return keep.tile([P, width], F32, name=name, tag="far_then_c%d" % r, align_bytes=64)
+
         for r in range(PACK):
             a = sb("a%d" % r, [P, T], F32)
-            nc.scalar.copy(out=a[:, 0:BANK], in_=banks[2 * r][:])
+            a_sb.append(a)
             if r == 0:
-                nc.vector.tensor_copy(out=a[:, BANK:T], in_=banks[2 * r + 1][:])
+                for k in range(4):
+                    cols = slice(k * QUARTER, (k + 1) * QUARTER)
+                    bank = psum.tile([P, QUARTER], F32, name="first%d" % k, offset=k * BANK_BYTES)
+                    nc.tensor.matmul_mx(
+                        out=bank[:],
+                        lhsT=q_codes[r].bitcast(FP8X4),
+                        lhsT_scale=q_plane[r],
+                        rhs=key_words[:, 2 * cols.start : 2 * cols.stop].bitcast(FP4X4),
+                        rhs_scale=key_plane[:, cols],
+                        start=True,
+                        stop=True,
+                    )
+                    if k % 2 == 0:
+                        nc.scalar.copy(out=a[:, cols], in_=bank[:])
+                    else:
+                        nc.vector.tensor_copy(out=a[:, cols], in_=bank[:])
             else:
-                nc.scalar.copy(out=a[:, BANK:T], in_=banks[2 * r + 1][:])
+                pair = scores(r)
+                nc.scalar.copy(out=a[:, 0:BANK], in_=pair[:, 0:BANK])
+                nc.scalar.copy(out=a[:, BANK:T], in_=pair[:, BANK:T])
             an = sb("a_near%d" % r, [P, I], F32)
-            af = sb("a_far%d" % r, [P, I], F32)
-            afl = sb("a_far_lam%d" % r, [P, I], F32)
+            af = shared("a_far%d" % r, r, I)
+            w = sb("w%d" % r, [P, I], F32)
             nc.scalar.activation(out=an[:], in_=a[:].indirect(near[:]), func=COPY)
             if r == 0:
                 nc.vector.tensor_copy(out=af[:], in_=a[:].indirect(far[:]))
-                nc.vector.tensor_scalar(out=afl[:], in0=af[:], scalar1=lam_sb[:, r : r + 1], scalar2=None, op0=ALU.mult)
             else:
                 nc.scalar.activation(out=af[:], in_=a[:].indirect(far[:]), func=COPY)
-                nc.scalar.activation(out=afl[:], in_=af[:], func=COPY, scale=lam_sb[:, r : r + 1])
+            nc.vector.scalar_tensor_tensor(
+                out=w[:], in0=af[:], scalar=lam_sb[:, r : r + 1], in1=an[:], op0=ALU.mult, op1=ALU.add
+            )
             f1 = placed[r % 2]
-            nc.vector.tensor_tensor(out=f1[:].indirect(place[:]), in0=afl[:], in1=an[:], op=ALU.add)
-            c = sb("c%d" % r, [P, T], F32)
-            nc.vector.tensor_tensor(out=c[:], in0=f1[:], in1=a[:], op=ALU.subtract)
+            if r > 0:
+                c = shared("c%d" % (r - 1), r, T)
+                nc.gpsimd.tensor_tensor(out=c[:], in0=placed[(r - 1) % 2][:], in1=a_sb[r - 1][:], op=ALU.subtract)
+                c1.append(c)
+            nc.vector.tensor_copy(out=f1[:].indirect(place[:]), in_=w[:])
             a_near.append(an)
-            c1.append(c)
+        c = sb("c_last", [P, T], F32)
+        f1 = placed[last % 2]
+        nc.vector.tensor_tensor(out=c[:, 0:BANK], in0=f1[:, 0:BANK], in1=pair[:, 0:BANK], op=ALU.subtract)
+        nc.vector.tensor_tensor(
+            out=c[:, BANK:SPLIT], in0=f1[:, BANK:SPLIT], in1=pair[:, BANK:SPLIT], op=ALU.subtract
+        )
+        nc.gpsimd.tensor_tensor(out=c[:, SPLIT:T], in0=f1[:, SPLIT:T], in1=a_sb[last][:, SPLIT:T], op=ALU.subtract)
+        c1.append(c)
 
-        last = PACK - 1
-        pieces = [(r, 0, I) for r in range(last)] + [(last, 0, HALF), (last, HALF, I)]
-        picked = []
-        for r, lo, hi in pieces:
-            cl = sb("c_left%d_%d" % (r, lo), [P, hi - lo], F32)
-            cr = sb("c_right%d_%d" % (r, lo), [P, hi - lo], F32)
-            nc.scalar.activation(out=cl[:], in_=c1[r][:].indirect(left[:, lo // 16 : hi // 16]), func=COPY)
-            nc.scalar.activation(out=cr[:], in_=c1[r][:].indirect(right[:, lo // 16 : hi // 16]), func=COPY)
-            picked.append((cl, cr))
         gw = sb("gw", [P, 2, PACK, HALF], BF16)
-        sums = []
-        for (r, lo, hi), (cl, cr) in zip(pieces, picked):
-            v = sb("v%d_%d" % (r, lo), [P, hi - lo], F32)
-            g = sb("g%d_%d" % (r, lo), [P, hi - lo], F32)
-            nc.vector.tensor_tensor(out=v[:], in0=cl[:], in1=cr[:], op=ALU.min)
-            nc.vector.tensor_tensor(out=g[:], in0=v[:], in1=a_near[r][:, lo:hi], op=ALU.add)
-            sums.append(g)
-        for (r, lo, hi), g in zip(pieces, sums):
-            if r < last:
-                nc.scalar.activation(
-                    out=gw[:, :, r, :],
-                    in_=g[:].rearrange("p (h i) -> p h i", h=2),
-                    func=COPY,
-                    scale=rowf_sb[:, r : r + 1],
-                )
+
+        def pick(r, lo, hi, lst, name, on_vector):
+            t = sb("%s%d_%d" % (name, r, lo), [P, hi - lo], F32)
+            src = c1[r][:].indirect(lst[:, lo // 16 : hi // 16])
+            if on_vector:
+                nc.vector.tensor_copy(out=t[:], in_=src)
             else:
-                nc.vector.tensor_scalar(
-                    out=gw[:, lo // HALF, r, :], in0=g[:], scalar1=rowf_sb[:, r : r + 1], scalar2=None, op0=ALU.mult
-                )
+                nc.scalar.activation(out=t[:], in_=src, func=COPY)
+            return t
+
+        def lower(r, lo, hi, cl, cr):
+            v = sb("v%d_%d" % (r, lo), [P, hi - lo], F32)
+            nc.vector.tensor_tensor(out=v[:], in0=cl[:], in1=cr[:], op=ALU.min)
+            return v
+
+        def add_near(r, lo, hi, v):
+            g = sb("g%d_%d" % (r, lo), [P, hi - lo], F32)
+            nc.vector.tensor_tensor(out=g[:], in0=v[:], in1=a_near[r][:, lo:hi], op=ALU.add)
+            return g
+
+        def scale(r, lo, hi, g, on_vector):
+            dst = gw[:, lo // HALF : hi // HALF, r, :]
+            src = g[:].rearrange("p (h i) -> p h i", i=HALF)
+            if on_vector:
+                nc.vector.tensor_scalar(out=dst, in0=src, scalar1=rowf_sb[:, r : r + 1], scalar2=None, op0=ALU.mult)
+            else:
+                nc.scalar.activation(out=dst, in_=src, func=COPY, scale=rowf_sb[:, r : r + 1])
+
+        pieces = [(r, 0, I) for r in range(last)] + [(last, 0, HALF), (last, HALF, I)]
+        picked = [(pick(*pc, left, "cl", False), pick(*pc, right, "cr", False)) for pc in pieces]
+        sums = [add_near(*pc, lower(*pc, *pk)) for pc, pk in zip(pieces, picked)]
+        for pc, g in zip(pieces, sums):
+            scale(*pc, g, pc[0] == last)
 
         woven = []
         for h in range(2):
@@ -187,7 +226,7 @@ def tile_attend_lookfar_one_mixed_kernel(
                 out=codes[:].bitcast(FP8X4), scales=plane[:], in_=woven[h][:].rearrange("p i r -> p (i r)")
             )
             for b in range(E // P):
-                bank = psum.tile([P, BANK], F32, name="bank")
+                bank = psum.tile([P, BANK], F32, name="bank%d_%d" % (h, b), offset=(4 + 2 * h + b) * BANK_BYTES)
                 nc.tensor.matmul_mx(
                     out=bank[:, 0:HALF],
                     lhsT=mix_codes[:, b * P : (b + 1) * P].bitcast(FP8X4),

@@ -22,6 +22,7 @@ BANK = 512
 HALF = I // 2
 LIST_COLS = I // 16
 SPLIT = 704
+WEAVE = 160
 BANK_BYTES = 2048
 QUARTER = T // 4
 
@@ -120,14 +121,22 @@ def tile_attend_lookfar_one_mixed_kernel(
             return pair
 
         last = PACK - 1
-        a_near, c1, a_sb = [], [], []
+        a_near, c1 = [], []
 
         def shared(name, r, width):
             return keep.tile([P, width], F32, name=name, tag="far_then_c%d" % r, align_bytes=64)
 
+        a_sb = [sb("a%d" % r, [P, T], F32) for r in range(PACK)]
+        pairs = {}
+
+        def leave_bank(r, h):
+            if h == 0:
+                pairs[r] = scores(r)
+            cols = slice(h * BANK, (h + 1) * BANK)
+            nc.scalar.copy(out=a_sb[r][:, cols], in_=pairs[r][:, cols])
+
         for r in range(PACK):
-            a = sb("a%d" % r, [P, T], F32)
-            a_sb.append(a)
+            a = a_sb[r]
             if r == 0:
                 for k in range(4):
                     cols = slice(k * QUARTER, (k + 1) * QUARTER)
@@ -146,29 +155,37 @@ def tile_attend_lookfar_one_mixed_kernel(
                     else:
                         nc.vector.tensor_copy(out=a[:, cols], in_=bank[:])
             else:
-                pair = scores(r)
-                nc.scalar.copy(out=a[:, 0:BANK], in_=pair[:, 0:BANK])
-                nc.scalar.copy(out=a[:, BANK:T], in_=pair[:, BANK:T])
+                if r == 1:
+                    leave_bank(r, 0)
+                if r < last:
+                    leave_bank(r, 1)
+                    leave_bank(r + 1, 0)
             an = sb("a_near%d" % r, [P, I], F32)
             af = shared("a_far%d" % r, r, I)
             w = sb("w%d" % r, [P, I], F32)
-            nc.scalar.activation(out=an[:], in_=a[:].indirect(near[:]), func=COPY)
-            if r == 0:
-                nc.vector.tensor_copy(out=af[:], in_=a[:].indirect(far[:]))
-            else:
-                nc.scalar.activation(out=af[:], in_=a[:].indirect(far[:]), func=COPY)
-            nc.vector.scalar_tensor_tensor(
-                out=w[:], in0=af[:], scalar=lam_sb[:, r : r + 1], in1=an[:], op0=ALU.mult, op1=ALU.add
-            )
             f1 = placed[r % 2]
-            if r > 0:
+            if r == 0:
+                nc.scalar.activation(out=an[:, 0:HALF], in_=a[:].indirect(near[:, 0 : HALF // 16]), func=COPY)
+                nc.vector.tensor_copy(out=af[:], in_=a[:].indirect(far[:]))
+                nc.vector.tensor_copy(out=an[:, HALF:I], in_=a[:].indirect(near[:, HALF // 16 : LIST_COLS]))
+                nc.vector.tensor_scalar(out=w[:], in0=af[:], scalar1=lam_sb[:, 0:1], scalar2=None, op0=ALU.mult)
+                nc.vector.tensor_tensor(out=f1[:].indirect(place[:]), in0=w[:], in1=an[:], op=ALU.add)
+            else:
+                nc.scalar.activation(out=an[:], in_=a[:].indirect(near[:]), func=COPY)
+                if r == last - 1:
+                    leave_bank(last, 1)
+                nc.scalar.activation(out=af[:], in_=a[:].indirect(far[:]), func=COPY)
+                nc.vector.scalar_tensor_tensor(
+                    out=w[:], in0=af[:], scalar=lam_sb[:, r : r + 1], in1=an[:], op0=ALU.mult, op1=ALU.add
+                )
                 c = shared("c%d" % (r - 1), r, T)
                 nc.gpsimd.tensor_tensor(out=c[:], in0=placed[(r - 1) % 2][:], in1=a_sb[r - 1][:], op=ALU.subtract)
                 c1.append(c)
-            nc.vector.tensor_copy(out=f1[:].indirect(place[:]), in_=w[:])
+                nc.vector.tensor_copy(out=f1[:].indirect(place[:]), in_=w[:])
             a_near.append(an)
         c = sb("c_last", [P, T], F32)
         f1 = placed[last % 2]
+        pair = pairs[last]
         nc.vector.tensor_tensor(out=c[:, 0:BANK], in0=f1[:, 0:BANK], in1=pair[:, 0:BANK], op=ALU.subtract)
         nc.vector.tensor_tensor(
             out=c[:, BANK:SPLIT], in0=f1[:, BANK:SPLIT], in1=pair[:, BANK:SPLIT], op=ALU.subtract
@@ -209,15 +226,16 @@ def tile_attend_lookfar_one_mixed_kernel(
         picked = [(pick(*pc, left, "cl", False), pick(*pc, right, "cr", False)) for pc in pieces]
         sums = [add_near(*pc, lower(*pc, *pk)) for pc, pk in zip(pieces, picked)]
         for pc, g in zip(pieces, sums):
-            scale(*pc, g, pc[0] == last)
+            scale(*pc, g, pc[0] >= 2)
 
         woven = []
         for h in range(2):
             w = sb("woven%d" % h, [P, HALF, PACK], BF16)
-            nc.vector.tensor_copy(
-                out=w[:].rearrange("p (c i) r -> p c r i", i=4),
-                in_=gw[:, h].rearrange("p r (c i) -> p c r i", i=4),
-            )
+            for weave, lo, hi in ((nc.vector.tensor_copy, 0, WEAVE), (nc.scalar.copy, WEAVE, HALF)):
+                weave(
+                    out=w[:, lo:hi, :].rearrange("p (c i) r -> p c r i", i=4),
+                    in_=gw[:, h, :, lo:hi].rearrange("p r (c i) -> p c r i", i=4),
+                )
             woven.append(w)
         for h in range(2):
             codes = sb("g_codes%d" % h, [P, HALF], U32)

from contextlib import ExitStack

import concourse.mybir as mybir

D, T, I, Q, E = 512, 1024, 512, 512, 256
FLOPS = 2 * D * Q * T + 2 * Q * E * I

F32 = mybir.dt.float32
BF16 = mybir.dt.bfloat16
I32 = mybir.dt.int32
U32 = mybir.dt.uint32
U16 = mybir.dt.uint16
U8 = mybir.dt.uint8
FP8X4 = mybir.dt.float8_e4m3fn_x4
FP4X4 = mybir.dt.float4_e2m1fn_x4
ALU = mybir.AluOpType
COPY = mybir.ActivationFunctionType.Copy

P = 128
PACK = 4
BANK = 512
HALF = I // 2
LIST_COLS = I // 16
SPLIT = 704
WEAVE = 160
BANK_BYTES = 2048
QUARTER = T // 4


def tile_attend_lookfar_one_mixed_kernel(
    tc, query, keys_words, keys_scales, lam, rowf, mix_words, mix_scales, offs, offs2, offs3, offs4, offs5, out
):
    nc = tc.nc
    with ExitStack() as ctx:
        keep = ctx.enter_context(tc.tile_pool(name="keep", bufs=1))
        psum = ctx.enter_context(tc.psum_pool(name="psum", bufs=1))

        def sb(name, shape, dtype):
            return keep.tile(shape, dtype, name=name, align_bytes=64)

        key_plane = sb("key_plane", [P, T], U8)
        mix_plane = sb("mix_plane", [P, E], U8)
        placed = [sb("placed%d" % b, [P, T], F32) for b in range(2)]
        nc.gpsimd.memset(key_plane[:].bitcast(I32), 0)
        nc.vector.memset(mix_plane[:].bitcast(I32), 0)
        for b in range(2):
            nc.vector.memset(placed[b][:], 0.0)

        for quad in range(4):
            nc.scalar.dma_start(
                out=key_plane[32 * quad : 32 * quad + 4, :].bitcast(I32),
                in_=keys_scales[0, 4 * quad : 4 * quad + 4, :].bitcast(I32),
            )
        q_rows = query.rearrange("(p j) q -> p j q", j=PACK)
        q_raw = []
        for c in range(2):
            raw = sb("q_raw%d" % c, [P, PACK, Q // 2], F32)
            nc.sync.dma_start(out=raw[:], in_=q_rows[:, :, c * (Q // 2) : (c + 1) * (Q // 2)])
            q_raw.append(raw)
        key_words = sb("key_words", [P, 2 * T], U8)
        nc.sync.dma_start(out=key_words[:].bitcast(I32), in_=keys_words[0].bitcast(I32))

        def load_list(name, src):
            tile = sb(name, [P, LIST_COLS], U16)
            nc.sync.dma_start(tile[:], src)
            return tile

        near = load_list("near", offs)
        far = load_list("far", offs2)
        lam_sb = sb("lam_sb", [P, PACK], F32)
        nc.sync.dma_start(out=lam_sb[:], in_=lam.rearrange("(p r) o -> p (r o)", r=PACK))
        place = load_list("place", offs3)
        left = load_list("left", offs4)
        right = load_list("right", offs5)
        rowf_sb = sb("rowf_sb", [P, PACK], F32)
        nc.sync.dma_start(out=rowf_sb[:], in_=rowf.rearrange("(p r) o -> p (r o)", r=PACK))
        mix_codes = sb("mix_codes", [P, E], U32)
        nc.sync.dma_start(out=mix_codes[:].bitcast(I32), in_=mix_words[0].rearrange("p n t -> p (n t)").bitcast(I32))
        for quad in range(4):
            nc.sync.dma_start(
                out=mix_plane[32 * quad : 32 * quad + 4, :].bitcast(I32),
                in_=mix_scales[0, 4 * quad : 4 * quad + 4, :].bitcast(I32),
            )

        q_bf = [sb("q_bf%d" % u, [P, 2, P, PACK], BF16) for u in range(2)]
        for c in range(2):
            src = q_raw[c][:].rearrange("p j (m r) -> p m j r", r=PACK)
            for u in range(2):
                dst = q_bf[u][:, :, c * 64 : (c + 1) * 64, :].rearrange("p r m j -> p m j r")
                if u == 0:
                    nc.vector.tensor_copy(out=dst, in_=src[:, :, :, 0:2])
                else:
                    nc.scalar.activation(out=dst, in_=src[:, :, :, 2:4], func=COPY)
        q_codes, q_plane = [], []
        for name, tiles in (("a", (0,)), ("b", (1,)), ("c", (2, 3))):
            n = len(tiles)
            codes = sb("q_codes_" + name, [P, n * P], U32)
            plane = sb("q_plane_" + name, [P, n * P], U8)
            u, first = divmod(tiles[0], 2)
            nc.vector.quantize_mx(
                out=codes[:].bitcast(FP8X4),
                scales=plane[:],
                in_=q_bf[u][:, first : first + n].rearrange("p r m j -> p (r m j)"),
            )
            for k in range(n):
                q_codes.append(codes[:, k * P : (k + 1) * P])
                q_plane.append(plane[:, k * P : (k + 1) * P])

        def scores(r):
            pair = psum.tile([P, T], F32, name="pair%d" % r, offset=2 * BANK_BYTES * ((r + 1) % 2))
            for h in range(2):
                nc.tensor.matmul_mx(
                    out=pair[:, BANK * h : BANK * (h + 1)],
                    lhsT=q_codes[r].bitcast(FP8X4),
                    lhsT_scale=q_plane[r],
                    rhs=key_words[:, 2 * BANK * h : 2 * BANK * (h + 1)].bitcast(FP4X4),
                    rhs_scale=key_plane[:, BANK * h : BANK * (h + 1)],
                    start=True,
                    stop=True,
                )
            return pair

        last = PACK - 1
        a_near, c1 = [], []

        def shared(name, r, width):
            return keep.tile([P, width], F32, name=name, tag="far_then_c%d" % r, align_bytes=64)

        a_sb = [sb("a%d" % r, [P, T], F32) for r in range(PACK)]
        pairs = {}

        def leave_bank(r, h):
            if h == 0:
                pairs[r] = scores(r)
            cols = slice(h * BANK, (h + 1) * BANK)
            nc.scalar.copy(out=a_sb[r][:, cols], in_=pairs[r][:, cols])

        for r in range(PACK):
            a = a_sb[r]
            if r == 0:
                for k in range(4):
                    cols = slice(k * QUARTER, (k + 1) * QUARTER)
                    bank = psum.tile([P, QUARTER], F32, name="first%d" % k, offset=k * BANK_BYTES)
                    nc.tensor.matmul_mx(
                        out=bank[:],
                        lhsT=q_codes[r].bitcast(FP8X4),
                        lhsT_scale=q_plane[r],
                        rhs=key_words[:, 2 * cols.start : 2 * cols.stop].bitcast(FP4X4),
                        rhs_scale=key_plane[:, cols],
                        start=True,
                        stop=True,
                    )
                    if k % 2 == 0:
                        nc.scalar.copy(out=a[:, cols], in_=bank[:])
                    else:
                        nc.vector.tensor_copy(out=a[:, cols], in_=bank[:])
            else:
                if r == 1:
                    leave_bank(r, 0)
                if r < last:
                    leave_bank(r, 1)
                    leave_bank(r + 1, 0)
            an = sb("a_near%d" % r, [P, I], F32)
            af = shared("a_far%d" % r, r, I)
            w = sb("w%d" % r, [P, I], F32)
            f1 = placed[r % 2]
            if r == 0:
                nc.scalar.activation(out=an[:, 0:HALF], in_=a[:].indirect(near[:, 0 : HALF // 16]), func=COPY)
                nc.vector.tensor_copy(out=af[:], in_=a[:].indirect(far[:]))
                nc.vector.tensor_copy(out=an[:, HALF:I], in_=a[:].indirect(near[:, HALF // 16 : LIST_COLS]))
                nc.vector.tensor_scalar(out=w[:], in0=af[:], scalar1=lam_sb[:, 0:1], scalar2=None, op0=ALU.mult)
                nc.vector.tensor_tensor(out=f1[:].indirect(place[:]), in0=w[:], in1=an[:], op=ALU.add)
            else:
                nc.scalar.activation(out=an[:], in_=a[:].indirect(near[:]), func=COPY)
                if r == last - 1:
                    leave_bank(last, 1)
                nc.scalar.activation(out=af[:], in_=a[:].indirect(far[:]), func=COPY)
                nc.vector.scalar_tensor_tensor(
                    out=w[:], in0=af[:], scalar=lam_sb[:, r : r + 1], in1=an[:], op0=ALU.mult, op1=ALU.add
                )
                c = shared("c%d" % (r - 1), r, T)
                nc.gpsimd.tensor_tensor(out=c[:], in0=placed[(r - 1) % 2][:], in1=a_sb[r - 1][:], op=ALU.subtract)
                c1.append(c)
                nc.vector.tensor_copy(out=f1[:].indirect(place[:]), in_=w[:])
            a_near.append(an)
        c = sb("c_last", [P, T], F32)
        f1 = placed[last % 2]
        pair = pairs[last]
        nc.vector.tensor_tensor(out=c[:, 0:BANK], in0=f1[:, 0:BANK], in1=pair[:, 0:BANK], op=ALU.subtract)
        nc.vector.tensor_tensor(
            out=c[:, BANK:SPLIT], in0=f1[:, BANK:SPLIT], in1=pair[:, BANK:SPLIT], op=ALU.subtract
        )
        nc.gpsimd.tensor_tensor(out=c[:, SPLIT:T], in0=f1[:, SPLIT:T], in1=a_sb[last][:, SPLIT:T], op=ALU.subtract)
        c1.append(c)

        gw = sb("gw", [P, 2, PACK, HALF], BF16)

        def pick(r, lo, hi, lst, name, on_vector):
            t = sb("%s%d_%d" % (name, r, lo), [P, hi - lo], F32)
            src = c1[r][:].indirect(lst[:, lo // 16 : hi // 16])
            if on_vector:
                nc.vector.tensor_copy(out=t[:], in_=src)
            else:
                nc.scalar.activation(out=t[:], in_=src, func=COPY)
            return t

        def lower(r, lo, hi, cl, cr):
            v = sb("v%d_%d" % (r, lo), [P, hi - lo], F32)
            nc.vector.tensor_tensor(out=v[:], in0=cl[:], in1=cr[:], op=ALU.min)
            return v

        def add_near(r, lo, hi, v):
            g = sb("g%d_%d" % (r, lo), [P, hi - lo], F32)
            nc.vector.tensor_tensor(out=g[:], in0=v[:], in1=a_near[r][:, lo:hi], op=ALU.add)
            return g

        def scale(r, lo, hi, g, on_vector):
            dst = gw[:, lo // HALF : hi // HALF, r, :]
            src = g[:].rearrange("p (h i) -> p h i", i=HALF)
            if on_vector:
                nc.vector.tensor_scalar(out=dst, in0=src, scalar1=rowf_sb[:, r : r + 1], scalar2=None, op0=ALU.mult)
            else:
                nc.scalar.activation(out=dst, in_=src, func=COPY, scale=rowf_sb[:, r : r + 1])

        pieces = [(r, 0, I) for r in range(last)] + [(last, 0, HALF), (last, HALF, I)]
        picked = [(pick(*pc, left, "cl", False), pick(*pc, right, "cr", False)) for pc in pieces]
        sums = [add_near(*pc, lower(*pc, *pk)) for pc, pk in zip(pieces, picked)]
        for pc, g in zip(pieces, sums):
            scale(*pc, g, pc[0] >= 2)

        woven = []
        for h in range(2):
            w = sb("woven%d" % h, [P, HALF, PACK], BF16)
            for weave, lo, hi in ((nc.vector.tensor_copy, 0, WEAVE), (nc.scalar.copy, WEAVE, HALF)):
                weave(
                    out=w[:, lo:hi, :].rearrange("p (c i) r -> p c r i", i=4),
                    in_=gw[:, h, :, lo:hi].rearrange("p r (c i) -> p c r i", i=4),
                )
            woven.append(w)
        for h in range(2):
            codes = sb("g_codes%d" % h, [P, HALF], U32)
            plane = sb("g_plane%d" % h, [P, HALF], U8)
            nc.vector.quantize_mx(
                out=codes[:].bitcast(FP8X4), scales=plane[:], in_=woven[h][:].rearrange("p i r -> p (i r)")
            )
            for b in range(E // P):
                bank = psum.tile([P, BANK], F32, name="bank%d_%d" % (h, b), offset=(4 + 2 * h + b) * BANK_BYTES)
                nc.tensor.matmul_mx(
                    out=bank[:, 0:HALF],
                    lhsT=mix_codes[:, b * P : (b + 1) * P].bitcast(FP8X4),
                    lhsT_scale=mix_plane[:, b * P : (b + 1) * P],
                    rhs=codes[:].bitcast(FP8X4),
                    rhs_scale=plane[:],
                    start=True,
                    stop=True,
                )
                y = sb("y%d_%d" % (h, b), [P, HALF], F32)
                dst = out[b * P : (b + 1) * P, h * HALF : (h + 1) * HALF]
                if h == 1 and b == 1:
                    nc.vector.tensor_copy(out=y[:], in_=bank[:, 0:HALF])
                    nc.sync.dma_start(out=dst, in_=y[:])
                else:
                    nc.scalar.copy(out=y[:], in_=bank[:, 0:HALF])
                    nc.sync.dma_start(out=dst, in_=y[:])
